import numpy as np
import ml_dtypes


def mxq(x, axis, fmt="e4m3"):
    dtype, down = {"e4m3": (ml_dtypes.float8_e4m3fn, 7), "e5m2": (ml_dtypes.float8_e5m2, 14)}[fmt]
    v = np.moveaxis(np.asarray(x, np.float32).astype(ml_dtypes.bfloat16).astype(np.float64), axis, -1)
    blocks = v.reshape(v.shape[:-1] + (-1, 32))
    amax = np.abs(blocks).max(-1, keepdims=True)
    byte = np.maximum(np.where(amax > 0, np.frexp(amax)[1] - 1 + 127, 0) - down, 1)
    scale = np.exp2(byte - 127.0)
    codes = (blocks / scale).astype(np.float32).astype(dtype).astype(np.float64)
    return np.moveaxis((codes * scale).reshape(v.shape), -1, axis)


WIDE = False


def mx_kscale(k):
    if not WIDE:
        return np.ones(k)
    levels = np.array([10, -10, 5, -5, 0])
    if k % 512:
        return np.exp2(np.random.permutation(np.resize(levels, k // 32))).repeat(32)
    a = np.empty((k // 512, 16))
    for p in range(k // 512):
        a[p, :8] = np.random.permutation(np.resize(levels, 8))
        for g in range(8):
            far = levels[np.abs(levels - a[p, g]) >= 10]
            a[p, g + 8] = far[np.random.randint(len(far))]
    return np.exp2(a.ravel()).repeat(32)


def f64(x):
    return np.asarray(x).astype(np.float64)


def striped(idx):
    return np.tile(idx.reshape(-1, 16).T, (8, 1)).astype(np.uint16)


def unstriped(offs):
    return offs[:16].T.reshape(-1).astype(np.int64)


E2M1 = np.array([0.0, 0.5, 1.0, 1.5, 2.0, 3.0, 4.0, 6.0, -0.0, -0.5, -1.0, -1.5, -2.0, -3.0, -4.0, -6.0])


def pack_weight(w, fmt):
    k, n = w.shape
    w = f64(np.asarray(w, np.float32).astype(ml_dtypes.bfloat16)).reshape(k // 32, 32, n)
    amax = np.abs(w).max(1)
    if fmt == "e4m3":
        byte = np.frexp(amax)[1] - 1 + 127 - 7
    else:
        mant, ex = np.frexp(amax / 6.0)
        byte = np.where(mant > 0.5, ex, ex - 1) + 127
    byte = np.clip(np.where(amax > 0, byte, 1), 1, 254)
    scaled = (w * np.exp2(127.0 - byte)[:, None, :]).reshape(k, n).astype(np.float32)
    by_word = np.ascontiguousarray(scaled.reshape(k // 512, 128, 4, n).transpose(0, 1, 3, 2))
    if fmt == "e4m3":
        words = by_word.astype(ml_dtypes.float8_e4m3fn).view(np.uint8)
    else:
        c = by_word.astype(ml_dtypes.float4_e2m1fn).view(np.uint8) & 0xF
        words = (c[..., 0::2] | (c[..., 1::2] << 4)).reshape(k // 512, 128, 2 * n)
    return np.ascontiguousarray(words), np.ascontiguousarray(byte.astype(np.uint8).reshape(k // 512, 16, n))


def unpack_weight(words, scales, fmt):
    g, _, n = scales.shape
    words = np.ascontiguousarray(words).reshape(g, 128, n, -1)
    if fmt == "e4m3":
        vals = words.view(ml_dtypes.float8_e4m3fn).astype(np.float64)
    else:
        nib = np.empty((g, 128, n, 4), np.uint8)
        nib[..., 0::2] = words & 0xF
        nib[..., 1::2] = words >> 4
        vals = E2M1[nib]
    vals = vals * np.repeat(np.exp2(scales.astype(np.float64) - 127.0), 8, axis=1)[..., None]
    return vals.transpose(0, 1, 3, 2).reshape(g * 512, n)


def gelu(v):
    return 0.5 * v * (1.0 + np.tanh(np.sqrt(2.0 / np.pi) * (v + 0.044715 * v**3)))


T, S, P, K, H, N = 4096, 1024, 512, 1024, 1024, 512

def setup_inputs():
    n = np.random.standard_normal
    s = mx_kscale(K)[:, None]
    u = mx_kscale(H)[:, None]
    d = {}
    d["tab_words"], d["tab_scales"] = pack_weight(n((K, T)) * s, "e2m1")
    d["offs"] = striped(np.random.permutation(T)[:S])
    d["pos1"] = striped(np.random.permutation(S)[:P])
    d["pos2"] = striped(np.random.permutation(S)[:P])
    d["w1"] = (0.56 * n((K, H)) / K ** 0.5 / s).astype(np.float32)
    d["gain"] = (np.exp(0.3 * n(H)) * u[:, 0]).astype(np.float32)
    d["w4_words"], d["w4_scales"] = pack_weight(3.0 * n((H, N)) / H ** 0.5 / u, "e2m1")
    return d

def reference(tab_words, tab_scales, offs, pos1, pos2, w1, gain, w4_words, w4_scales):
    v = unpack_weight(tab_words, tab_scales, "e2m1")[:, unstriped(offs)]
    h = mxq(f64(w1), 0, "e4m3").T @ v
    treble = np.tanh(h[:, unstriped(pos1)])
    tenor = np.sin(h[:, unstriped(pos2)])
    z = (treble - tenor) * f64(gain)[:, None]
    zq = mxq(z, 0, "e4m3")
    w4 = unpack_weight(w4_words, w4_scales, "e2m1")
    y = w4.T @ zq
    return np.sqrt(np.square(y) + 1.0)

@@ -1,0 +1,328 @@
+import math
+from contextlib import ExitStack
+
+import concourse.mybir as mybir
+
+T, S, M, K, H, N = 4096, 1024, 512, 1024, 1024, 512
+FLOPS = 2 * K * H * S + 2 * H * N * M
+
+F32 = mybir.dt.float32
+BF16 = mybir.dt.bfloat16
+I32 = mybir.dt.int32
+U32 = mybir.dt.uint32
+U16 = mybir.dt.uint16
+U8 = mybir.dt.uint8
+FP8X4 = mybir.dt.float8_e4m3fn_x4
+FP4X4 = mybir.dt.float4_e2m1fn_x4
+ACT = mybir.ActivationFunctionType
+ALU = mybir.AluOpType
+
+P = 128
+PACK = 4
+PASS = P * PACK
+BANK = 512
+QUARTER = 128
+
+CHUNKS = [(0, 0, 512, True), (1, 0, 256, True), (1, 256, 128, False), (1, 384, 128, False)]
+
+
+def tile_list_string_unison_beats_kernel(
+    tc, tab_words, tab_scales, offs, pos1, pos2, w1, gain, w4_words, w4_scales, out
+):
+    nc = tc.nc
+    with ExitStack() as ctx:
+        held = ctx.enter_context(tc.tile_pool(name="held", bufs=1))
+        hpsum = ctx.enter_context(tc.psum_pool(name="hpsum", bufs=4))
+        ypsum = ctx.enter_context(tc.psum_pool(name="ypsum", bufs=1))
+
+        offs_t = held.tile([P, S // 16], U16, name="offs_t")
+        pos1_t = held.tile([P, M // 16], U16, name="pos1_t")
+        pos2_t = held.tile([P, M // 16], U16, name="pos2_t")
+        tabw = [held.tile([P, T], U16, name="tabw%d" % a, tag="tabw%d" % a, align_bytes=64) for a in range(2)]
+        tabs = held.tile([P, T], U8, name="tabs", tag="tabs", align_bytes=64)
+        vw = [held.tile([P, S], U16, name="vw%d" % a, align_bytes=64) for a in range(2)]
+        picked = held.tile([P, S], U8, name="picked", align_bytes=64)
+        vs = held.tile([P, 2, S], U8, name="vs", align_bytes=64)
+        warm = held.tile([P, 2], F32, name="warm")
+
+        nc.vector.memset(warm[:, 0:1], 0.0)
+        nc.vector.memset(tabs[32:64, :].bitcast(I32), 0)
+        nc.vector.memset(tabs[64:128, :].bitcast(I32), 0)
+        nc.vector.memset(vs[:].rearrange("p a n -> p (a n)").bitcast(I32), 0)
+        nc.scalar.activation(warm[:, 1:2], warm[:, 0:1], ACT.Silu)
+
+        pieces = [(0, 0, 0, 128), (0, 1, 0, 96), (0, 1, 96, 32), (1, 0, 0, 128), (1, 1, 0, 128)]
+        wraw = {}
+
+        def load_w(piece, tag):
+            b, a, m0, mc = piece
+            raw = held.tile([P, PACK, PACK * mc], F32, name="wraw%d%d%d" % (b, a, m0), tag=tag, align_bytes=64)
+            c0 = PASS * b + PACK * m0
+            rows = w1[PASS * a : PASS * (a + 1), c0 : c0 + PACK * mc]
+            nc.sync.dma_start(out=raw[:], in_=rows.rearrange("(p j) c -> p j c", j=PACK))
+            wraw[piece] = raw
+
+        nc.sync.dma_start(offs_t[:], offs)
+        nc.sync.dma_start(pos2_t[:], pos2)
+        nc.sync.dma_start(pos1_t[:], pos1)
+        nc.sync.dma_start(out=tabs[0:32, :].bitcast(I32), in_=tab_scales.rearrange("a q t -> q a t").bitcast(I32))
+        for a in range(2):
+            nc.sync.dma_start(out=tabw[a][:].bitcast(I32), in_=tab_words[a].bitcast(I32))
+        for n in range(3):
+            load_w(pieces[n], "wraw%d" % n)
+
+        wb, wq = {}, {}
+        reuse = {(1, 0): "wq011", (1, 1): "wq012"}
+        ws = {(b, a): held.tile([P, PASS], U8, name="ws%d%d" % (b, a), align_bytes=64)
+              for b in range(2) for a in range(2)}
+
+        def cast_w(piece, on_vector, lo, hi):
+            b, a, m0, mc = piece
+            if (b, a) not in wb:
+                wb[b, a] = held.tile([P, PACK, P, PACK], BF16, name="wb%d%d" % (b, a),
+                                     tag=reuse.get((b, a), "wb%d%d" % (b, a)), align_bytes=64)
+            dst = wb[b, a][:, :, m0 + lo : m0 + hi, :].rearrange("p t m j -> p m j t")
+            src = wraw[piece][:, :, PACK * lo : PACK * hi].rearrange("p j (m t) -> p m j t", t=PACK)
+            if on_vector:
+                nc.vector.tensor_copy(out=dst, in_=src)
+            else:
+                nc.scalar.copy(out=dst, in_=src)
+
+        def quantize_w(b, a, t0, t1):
+            name = "wq%d%d%d" % (b, a, t0)
+            codes = held.tile([P, P * (t1 - t0)], U32, name=name, tag=name, align_bytes=64)
+            for t in range(t0, t1):
+                wq[b, a, t] = codes[:, P * (t - t0) : P * (t - t0 + 1)]
+            nc.vector.quantize_mx(
+                out=codes[:].bitcast(FP8X4),
+                scales=ws[b, a][:, P * t0 : P * t1],
+                in_=wb[b, a][:, t0:t1, :, :].rearrange("p t m j -> p (t m j)"),
+            )
+
+        nc.vector.tensor_copy(picked[:], tabs[:].indirect(offs_t[:]))
+        for q in range(4):
+            nc.scalar.dma_start(out=vs[32 * q : 32 * q + 4, :, :].bitcast(I32), in_=picked[8 * q : 8 * q + 8, :].bitcast(I32))
+        for a in range(2):
+            nc.vector.tensor_copy(vw[a][:], tabw[a][:].indirect(offs_t[:]))
+        load_w(pieces[3], "tabw0")
+        load_w(pieces[4], "tabw1")
+        w4w = held.tile([P, 2, 2 * N], U8, name="w4w", tag="wraw0", align_bytes=64)
+        cast_w(pieces[0], False, 0, 64)
+        cast_w(pieces[0], True, 64, 128)
+        nc.sync.dma_start(out=w4w[:].bitcast(I32), in_=w4_words.rearrange("a p c -> p a c").bitcast(I32))
+        cast_w(pieces[1], False, 0, 48)
+        cast_w(pieces[1], True, 48, 96)
+        quantize_w(0, 0, 0, 4)
+        cast_w(pieces[2], True, 0, 32)
+        for t in range(PACK):
+            quantize_w(0, 1, t, t + 1)
+
+        gain_t = held.tile([P, 2, PACK], F32, name="gain_t", tag="wraw1", align_bytes=64)
+        w4s = held.tile([P, 2, N], U8, name="w4s", tag="wraw2", align_bytes=64)
+        nc.vector.memset(w4s[:].rearrange("p a n -> p (a n)").bitcast(I32), 0)
+        nc.sync.dma_start(out=gain_t[:], in_=gain.rearrange("(a p i) -> p a i", a=2, i=PACK))
+        for q in range(4):
+            nc.sync.dma_start(
+                out=w4s[32 * q : 32 * q + 4, :, :].bitcast(I32),
+                in_=w4_scales[:, 4 * q : 4 * q + 4, :].rearrange("a r n -> r a n").bitcast(I32),
+            )
+
+        h = {}
+
+        def make_h(b, t):
+            tile = held.tile([P, S], F32, name="h%d%d" % (b, t), tag="h%d%d" % (b, t), align_bytes=64)
+            for half in range(2):
+                cols = slice(BANK * half, BANK * (half + 1))
+                acc = hpsum.tile([P, BANK], F32, name="hacc")
+                for a in range(2):
+                    nc.tensor.matmul_mx(
+                        out=acc[:],
+                        lhsT=wq[b, a, t].bitcast(FP8X4),
+                        lhsT_scale=ws[b, a][:, P * t : P * (t + 1)],
+                        rhs=vw[a][:, cols].bitcast(FP4X4),
+                        rhs_scale=vs[:, a, cols],
+                        start=(a == 0),
+                        stop=(a == 1),
+                    )
+                if (b, t, half) == (0, 0, 1):
+                    nc.vector.tensor_copy(out=tile[:, cols], in_=acc[:])
+                else:
+                    nc.scalar.copy(out=tile[:, cols], in_=acc[:])
+            h[b, t] = tile
+
+        zq = [held.tile([P, M], U32, name="zq%d" % a, align_bytes=64) for a in range(2)]
+        zs = [held.tile([P, M], U8, name="zs%d" % a, align_bytes=64) for a in range(2)]
+        ybank = [ypsum.tile([P, N // P, QUARTER], F32, name="y%d" % q) for q in range(M // QUARTER)]
+        treble, tenor, frac = {}, {}, {}
+        last = len(CHUNKS) - 1
+
+        def gather_tenor(c, i):
+            a, m0, mc, unused = CHUNKS[c]
+            if i == 0:
+                tenor[c] = held.tile([P, PACK, mc], F32, name="tenor%d" % c, tag=["tenor0", "tenor1", "tenor0", "zb1"][c], align_bytes=64)
+            nc.vector.tensor_copy(tenor[c][:, i, :], h[a, i][:].indirect(pos2_t[:, m0 // 16 : (m0 + mc) // 16]))
+
+        def gather_treble(c, i):
+            a, m0, mc, unused = CHUNKS[c]
+            if i == 0:
+                treble[c] = held.tile([P, PACK, mc], F32, name="treble%d" % c, tag=["treble0", "treble1", "tenor1", "diff1"][c], align_bytes=64)
+            nc.vector.tensor_copy(treble[c][:, i, :], h[a, i][:].indirect(pos1_t[:, m0 // 16 : (m0 + mc) // 16]))
+
+        turns = {}
+
+        def count_turns(c, i0, i1):
+            mc = CHUNKS[c][2]
+            if i0 == 0:
+                turns[c] = held.tile([P, PACK, mc], I32, name="turns%d" % c)
+            nc.vector.tensor_scalar(
+                out=turns[c][:, i0:i1, :], in0=tenor[c][:, i0:i1, :],
+                scalar1=1.0 / (2.0 * math.pi), scalar2=None, op0=ALU.mult,
+            )
+
+        def reduce_turns(c, i0, i1):
+            mc = CHUNKS[c][2]
+            if i0 == 0:
+                frac[c] = held.tile([P, PACK, mc], F32, name="frac%d" % c, tag="frac%d" % c)
+            nc.vector.scalar_tensor_tensor(
+                out=frac[c][:, i0:i1, :], in0=tenor[c][:, i0:i1, :], scalar=1.0 / (2.0 * math.pi),
+                in1=turns[c][:, i0:i1, :], op0=ALU.mult, op1=ALU.subtract,
+            )
+
+        def do_tanh(c, i0, i1):
+            nc.scalar.activation(treble[c][:, i0:i1, :], treble[c][:, i0:i1, :], ACT.Tanh)
+
+        def do_sin(c, i0, i1):
+            nc.scalar.activation(tenor[c][:, i0:i1, :], frac[c][:, i0:i1, :], ACT.Sin, scale=2.0 * math.pi)
+
+        def scale_sin(c, i0, i1):
+            a, m0, mc, on_scalar = CHUNKS[c]
+            if on_scalar:
+                for i in range(i0, i1):
+                    nc.scalar.activation(tenor[c][:, i, :], tenor[c][:, i, :], ACT.Copy, scale=gain_t[:, a, i : i + 1])
+
+        diff, zb = {}, {}
+
+        def difference(c, i0, i1):
+            a, m0, mc, on_scalar = CHUNKS[c]
+            if i0 == 0:
+                diff[c] = held.tile([P, PACK, mc], F32, name="diff%d" % c, tag="h13" if c == last - 1 else "diff%d" % c, align_bytes=64)
+            if on_scalar:
+                for i in range(i0, i1):
+                    nc.vector.scalar_tensor_tensor(
+                        out=diff[c][:, i, :], in0=treble[c][:, i, :], scalar=gain_t[:, a, i : i + 1],
+                        in1=tenor[c][:, i, :], op0=ALU.mult, op1=ALU.subtract,
+                    )
+            else:
+                nc.vector.tensor_tensor(diff[c][:, i0:i1, :], treble[c][:, i0:i1, :], tenor[c][:, i0:i1, :], ALU.subtract)
+
+        def interleave(c):
+            a, m0, mc, on_scalar = CHUNKS[c]
+            zb[c] = held.tile([P, mc, PACK], BF16, name="zb%d" % c, tag="zb%d" % c, align_bytes=64)
+            dst = zb[c][:].rearrange("p (c u) i -> p c i u", u=4)
+            src = diff[c][:].rearrange("p i (c u) -> p c i u", u=4)
+            if on_scalar:
+                nc.scalar.copy(out=dst, in_=src)
+            else:
+                g = gain_t[:, a, :].rearrange("p (c i u) -> p c i u", c=1, u=1).broadcast_to([P, mc // 4, PACK, 4])
+                nc.vector.tensor_tensor(dst, src, g, ALU.mult)
+
+        def second_product(c):
+            a, m0, mc, unused = CHUNKS[c]
+            nc.vector.quantize_mx(
+                out=zq[a][:, m0 : m0 + mc].bitcast(FP8X4),
+                scales=zs[a][:, m0 : m0 + mc],
+                in_=zb[c][:].rearrange("p m i -> p (m i)"),
+            )
+            for q in range(m0 // QUARTER, (m0 + mc) // QUARTER):
+                cols = slice(QUARTER * q, QUARTER * (q + 1))
+                for n in range(N // P):
+                    nc.tensor.matmul_mx(
+                        out=ybank[q][:, n, :],
+                        lhsT=w4w[:, a, 2 * P * n : 2 * P * (n + 1)].bitcast(FP4X4),
+                        lhsT_scale=w4s[:, a, P * n : P * (n + 1)],
+                        rhs=zq[a][:, cols].bitcast(FP8X4),
+                        rhs_scale=zs[a][:, cols],
+                        start=(a == 0 and n == 0),
+                        stop=(a == 1 and n == N // P - 1),
+                    )
+
+        squares = held.tile([P, M // QUARTER, BANK], F32, name="squares")
+
+        def square(q):
+            nc.scalar.activation(squares[:, q, :], ybank[q][:].rearrange("p n m -> p (n m)"), ACT.Square)
+
+        def gather_both(c, i):
+            gather_tenor(c, i)
+            gather_treble(c, i)
+
+        for t in range(2):
+            make_h(0, t)
+            gather_both(0, t)
+        count_turns(0, 0, 2)
+        cast_w(pieces[3], False, 0, 128)
+        quantize_w(1, 0, 0, 4)
+        reduce_turns(0, 0, 2)
+        make_h(0, 2)
+        gather_both(0, 2)
+        cast_w(pieces[4], False, 0, 128)
+        quantize_w(1, 1, 0, 2)
+        quantize_w(1, 1, 2, 4)
+        make_h(0, 3)
+        gather_both(0, 3)
+        count_turns(0, 2, 4)
+        do_sin(0, 0, 2)
+        do_tanh(0, 0, 2)
+        scale_sin(0, 0, 2)
+        reduce_turns(0, 2, 4)
+        difference(0, 0, 2)
+        for t in range(PACK):
+            make_h(1, t)
+            gather_both(1, t)
+        do_sin(0, 2, 4)
+        do_tanh(0, 2, 4)
+        scale_sin(0, 2, 4)
+        count_turns(1, 0, 4)
+        difference(0, 2, 4)
+        reduce_turns(1, 0, 4)
+        do_tanh(1, 0, 4)
+        do_sin(1, 0, 4)
+        interleave(0)
+        scale_sin(1, 0, 4)
+        for t in range(PACK):
+            gather_tenor(2, t)
+        count_turns(2, 0, 4)
+        second_product(0)
+        reduce_turns(2, 0, 4)
+        do_sin(2, 0, 4)
+        difference(1, 0, 4)
+        interleave(1)
+        for t in range(PACK):
+            gather_treble(2, t)
+        do_tanh(2, 0, 4)
+        second_product(1)
+        square(0)
+        square(1)
+        for t in range(PACK):
+            gather_tenor(3, t)
+        count_turns(3, 0, 4)
+        gather_treble(3, 0)
+        reduce_turns(3, 0, 4)
+        for t in range(1, PACK):
+            gather_treble(3, t)
+        do_sin(3, 0, 4)
+        do_tanh(3, 0, 4)
+        difference(2, 0, 4)
+        interleave(2)
+        difference(last, 0, 4)
+        second_product(last - 1)
+        interleave(last)
+        square(2)
+        second_product(last)
+
+        result = held.tile([P, M // QUARTER, N // P, QUARTER], F32, name="result", tag="frac%d" % last)
+        out_view = out.rearrange("(n p) m -> p n m", p=P)
+        for q in range(M // QUARTER):
+            if q == M // QUARTER - 1:
+                square(q)
+            nc.scalar.activation(result[:, q].rearrange("p n m -> p (n m)"), squares[:, q, :], ACT.Sqrt, bias=1.0)
+            nc.sync.dma_start(out=out_view[:, :, QUARTER * q : QUARTER * (q + 1)], in_=result[:, q])

@@ -150,7 +150,7 @@ def tile_list_string_unison_beats_kernel(
                     nc.scalar.copy(out=tile[:, cols], in_=acc[:])
             h[b, t] = tile
 
-        zq = [held.tile([P, M], U32, name="zq%d" % a, align_bytes=64) for a in range(2)]
+        zq = {}
         zs = [held.tile([P, M], U8, name="zs%d" % a, align_bytes=64) for a in range(2)]
         ybank = [ypsum.tile([P, N // P, QUARTER], F32, name="y%d" % q) for q in range(M // QUARTER)]
         treble, tenor, frac = {}, {}, {}
@@ -159,33 +159,34 @@ def tile_list_string_unison_beats_kernel(
         def gather_tenor(c, i):
             a, m0, mc, unused = CHUNKS[c]
             if i == 0:
-                tenor[c] = held.tile([P, PACK, mc], F32, name="tenor%d" % c, tag=["tenor0", "tenor1", "tenor0", "zb1"][c], align_bytes=64)
+                both = held.tile([P, 2, PACK, mc], F32, name="both%d" % c, tag=["both0", "both1", "turns1b", "zb1"][c], align_bytes=64)
+                tenor[c], treble[c] = both[:, 0], both[:, 1]
             nc.vector.tensor_copy(tenor[c][:, i, :], h[a, i][:].indirect(pos2_t[:, m0 // 16 : (m0 + mc) // 16]))
 
         def gather_treble(c, i):
             a, m0, mc, unused = CHUNKS[c]
-            if i == 0:
-                treble[c] = held.tile([P, PACK, mc], F32, name="treble%d" % c, tag=["treble0", "treble1", "tenor1", "diff1"][c], align_bytes=64)
             nc.vector.tensor_copy(treble[c][:, i, :], h[a, i][:].indirect(pos1_t[:, m0 // 16 : (m0 + mc) // 16]))
 
         turns = {}
 
         def count_turns(c, i0, i1):
             mc = CHUNKS[c][2]
-            if i0 == 0:
-                turns[c] = held.tile([P, PACK, mc], I32, name="turns%d" % c)
-            nc.vector.tensor_scalar(
-                out=turns[c][:, i0:i1, :], in0=tenor[c][:, i0:i1, :],
-                scalar1=1.0 / (2.0 * math.pi), scalar2=None, op0=ALU.mult,
+            name = "turns%d%s" % (c, "" if i0 == 0 else "b" if i0 == 2 else "c")
+            part = held.tile([P, i1 - i0, mc], I32, name=name, tag=name, align_bytes=64)
+            turns[c, i0] = part
+            engine = nc.vector if c == last else nc.gpsimd
+            engine.tensor_scalar(
+                out=part[:], in0=tenor[c][:, i0:i1, :],
+                scalar1=1.0 / (2.0 * math.pi), scalar2=0.0, op0=ALU.mult, op1=ALU.add,
             )
 
         def reduce_turns(c, i0, i1):
             mc = CHUNKS[c][2]
             if i0 == 0:
-                frac[c] = held.tile([P, PACK, mc], F32, name="frac%d" % c, tag="frac%d" % c)
+                frac[c] = held.tile([P, PACK, mc], F32, name="frac%d" % c, tag="both1" if c == 2 else "frac%d" % c, align_bytes=64)
             nc.vector.scalar_tensor_tensor(
                 out=frac[c][:, i0:i1, :], in0=tenor[c][:, i0:i1, :], scalar=1.0 / (2.0 * math.pi),
-                in1=turns[c][:, i0:i1, :], op0=ALU.mult, op1=ALU.subtract,
+                in1=turns[c, i0][:], op0=ALU.mult, op1=ALU.subtract,
             )
 
         def do_tanh(c, i0, i1):
@@ -228,12 +229,16 @@ def tile_list_string_unison_beats_kernel(
 
         def second_product(c):
             a, m0, mc, unused = CHUNKS[c]
+            if a not in zq:
+                zq[a] = held.tile([P, M], U32, name="zq%d" % a, tag="turns2" if a == 0 else "zq1", align_bytes=64)
             nc.vector.quantize_mx(
                 out=zq[a][:, m0 : m0 + mc].bitcast(FP8X4),
                 scales=zs[a][:, m0 : m0 + mc],
                 in_=zb[c][:].rearrange("p m i -> p (m i)"),
             )
-            for q in range(m0 // QUARTER, (m0 + mc) // QUARTER):
+
+        def multiply(a, quarters):
+            for q in quarters:
                 cols = slice(QUARTER * q, QUARTER * (q + 1))
                 for n in range(N // P):
                     nc.tensor.matmul_mx(
@@ -255,10 +260,12 @@ def tile_list_string_unison_beats_kernel(
             gather_tenor(c, i)
             gather_treble(c, i)
 
-        for t in range(2):
-            make_h(0, t)
-            gather_both(0, t)
+        make_h(0, 0)
+        gather_both(0, 0)
+        make_h(0, 1)
+        gather_tenor(0, 1)
         count_turns(0, 0, 2)
+        gather_treble(0, 1)
         cast_w(pieces[3], False, 0, 128)
         quantize_w(1, 0, 0, 4)
         reduce_turns(0, 0, 2)
@@ -268,38 +275,52 @@ def tile_list_string_unison_beats_kernel(
         quantize_w(1, 1, 0, 2)
         quantize_w(1, 1, 2, 4)
         make_h(0, 3)
-        gather_both(0, 3)
+        gather_tenor(0, 3)
         count_turns(0, 2, 4)
+        gather_treble(0, 3)
         do_sin(0, 0, 2)
         do_tanh(0, 0, 2)
         scale_sin(0, 0, 2)
         reduce_turns(0, 2, 4)
         difference(0, 0, 2)
-        for t in range(PACK):
+        for t in range(2):
             make_h(1, t)
-            gather_both(1, t)
+            gather_tenor(1, t)
+            if t == 1:
+                count_turns(1, 0, 2)
+            gather_treble(1, t)
         do_sin(0, 2, 4)
         do_tanh(0, 2, 4)
         scale_sin(0, 2, 4)
-        count_turns(1, 0, 4)
         difference(0, 2, 4)
-        reduce_turns(1, 0, 4)
-        do_tanh(1, 0, 4)
-        do_sin(1, 0, 4)
+        for t in range(2, PACK):
+            make_h(1, t)
+            gather_tenor(1, t)
+            if t == 3:
+                count_turns(1, 2, 4)
+            gather_treble(1, t)
+        reduce_turns(1, 0, 2)
+        reduce_turns(1, 2, 4)
         interleave(0)
-        scale_sin(1, 0, 4)
+        for i in (0, 2):
+            do_sin(1, i, i + 2)
+            do_tanh(1, i, i + 2)
+            scale_sin(1, i, i + 2)
         for t in range(PACK):
             gather_tenor(2, t)
         count_turns(2, 0, 4)
-        second_product(0)
-        reduce_turns(2, 0, 4)
-        do_sin(2, 0, 4)
-        difference(1, 0, 4)
-        interleave(1)
         for t in range(PACK):
             gather_treble(2, t)
+        difference(1, 0, 4)
         do_tanh(2, 0, 4)
+        interleave(1)
+        reduce_turns(2, 0, 4)
+        do_sin(2, 0, 4)
+        second_product(0)
+        multiply(0, (0, 1))
         second_product(1)
+        multiply(1, (0, 1))
+        multiply(0, (2, 3))
         square(0)
         square(1)
         for t in range(PACK):
@@ -315,11 +336,13 @@ def tile_list_string_unison_beats_kernel(
         interleave(2)
         difference(last, 0, 4)
         second_product(last - 1)
+        multiply(1, (2,))
         interleave(last)
         square(2)
         second_product(last)
+        multiply(1, (3,))
 
-        result = held.tile([P, M // QUARTER, N // P, QUARTER], F32, name="result", tag="frac%d" % last)
+        result = held.tile([P, M // QUARTER, N // P, QUARTER], F32, name="result", tag="frac%d" % last, align_bytes=64)
         out_view = out.rearrange("(n p) m -> p n m", p=P)
         for q in range(M // QUARTER):
             if q == M // QUARTER - 1:

@@ -18,6 +18,8 @@ ACT = mybir.ActivationFunctionType
 ALU = mybir.AluOpType
 
 P = 128
+TREBLE_TAG = ["treble0", None, "treble11", "treble12"]
+DIFF_TAG = ["diff0", "diff1", "zb1", "diff3"]
 PACK = 4
 PASS = P * PACK
 BANK = 512
@@ -51,7 +53,7 @@ def tile_list_string_unison_beats_kernel(
         nc.vector.memset(vs[:].rearrange("p a n -> p (a n)").bitcast(I32), 0)
         nc.scalar.activation(warm[:, 1:2], warm[:, 0:1], ACT.Silu)
 
-        pieces = [(0, 0, 0, 128), (0, 1, 0, 96), (0, 1, 96, 32), (1, 0, 0, 128), (1, 1, 0, 128)]
+        pieces = [(0, 0, 0, 128), (0, 1, 0, 64), (0, 1, 64, 64), (1, 0, 0, 128), (1, 1, 0, 128)]
         wraw = {}
 
         def load_w(piece, tag):
@@ -81,8 +83,8 @@ def tile_list_string_unison_beats_kernel(
             if (b, a) not in wb:
                 wb[b, a] = held.tile([P, PACK, P, PACK], BF16, name="wb%d%d" % (b, a),
                                      tag=reuse.get((b, a), "wb%d%d" % (b, a)), align_bytes=64)
-            dst = wb[b, a][:, :, m0 + lo : m0 + hi, :].rearrange("p t m j -> p m j t")
-            src = wraw[piece][:, :, PACK * lo : PACK * hi].rearrange("p j (m t) -> p m j t", t=PACK)
+            dst = wb[b, a][:, :, m0 + lo : m0 + hi, :].rearrange("p t m j -> p m t j")
+            src = wraw[piece][:, :, PACK * lo : PACK * hi].rearrange("p j (m t) -> p m t j", t=PACK)
             if on_vector:
                 nc.vector.tensor_copy(out=dst, in_=src)
             else:
@@ -107,13 +109,13 @@ def tile_list_string_unison_beats_kernel(
         load_w(pieces[3], "tabw0")
         load_w(pieces[4], "tabw1")
         w4w = held.tile([P, 2, 2 * N], U8, name="w4w", tag="wraw0", align_bytes=64)
-        cast_w(pieces[0], False, 0, 64)
-        cast_w(pieces[0], True, 64, 128)
+        cast_w(pieces[0], False, 0, 80)
+        cast_w(pieces[0], True, 80, 128)
         nc.sync.dma_start(out=w4w[:].bitcast(I32), in_=w4_words.rearrange("a p c -> p a c").bitcast(I32))
-        cast_w(pieces[1], False, 0, 48)
-        cast_w(pieces[1], True, 48, 96)
+        cast_w(pieces[1], False, 0, 64)
         quantize_w(0, 0, 0, 4)
-        cast_w(pieces[2], True, 0, 32)
+        cast_w(pieces[2], False, 0, 32)
+        cast_w(pieces[2], True, 32, 64)
         for t in range(PACK):
             quantize_w(0, 1, t, t + 1)
 
@@ -153,68 +155,70 @@ def tile_list_string_unison_beats_kernel(
         zq = {}
         zs = [held.tile([P, M], U8, name="zs%d" % a, align_bytes=64) for a in range(2)]
         ybank = [ypsum.tile([P, N // P, QUARTER], F32, name="y%d" % q) for q in range(M // QUARTER)]
-        treble, tenor, frac = {}, {}, {}
         last = len(CHUNKS) - 1
+        tenor = [held.tile([P, PACK, M], F32, name="tenor%d" % a) for a in range(2)]
+        turns, frac, treble, diff, zb = {}, {}, {}, {}, {}
 
-        def gather_tenor(c, i):
-            a, m0, mc, unused = CHUNKS[c]
-            if i == 0:
-                both = held.tile([P, 2, PACK, mc], F32, name="both%d" % c, tag=["both0", "both1", "turns1b", "zb1"][c], align_bytes=64)
-                tenor[c], treble[c] = both[:, 0], both[:, 1]
-            nc.vector.tensor_copy(tenor[c][:, i, :], h[a, i][:].indirect(pos2_t[:, m0 // 16 : (m0 + mc) // 16]))
-
-        def gather_treble(c, i):
-            a, m0, mc, unused = CHUNKS[c]
-            nc.vector.tensor_copy(treble[c][:, i, :], h[a, i][:].indirect(pos1_t[:, m0 // 16 : (m0 + mc) // 16]))
-
-        turns = {}
-
-        def count_turns(c, i0, i1):
-            mc = CHUNKS[c][2]
-            name = "turns%d%s" % (c, "" if i0 == 0 else "b" if i0 == 2 else "c")
-            part = held.tile([P, i1 - i0, mc], I32, name=name, tag=name, align_bytes=64)
-            turns[c, i0] = part
-            engine = nc.vector if c == last else nc.gpsimd
-            engine.tensor_scalar(
-                out=part[:], in0=tenor[c][:, i0:i1, :],
+        def gather_tenor(a, i):
+            nc.vector.tensor_copy(tenor[a][:, i, :], h[a, i][:].indirect(pos2_t[:]))
+            name = "turns%d%d" % (a, i // 2)
+            if i % 2 == 0:
+                turns[a, i // 2] = held.tile([P, 2, M], I32, name=name, tag=name, align_bytes=64)
+            nc.gpsimd.tensor_scalar(
+                out=turns[a, i // 2][:, i % 2, :], in0=tenor[a][:, i, :],
                 scalar1=1.0 / (2.0 * math.pi), scalar2=0.0, op0=ALU.mult, op1=ALU.add,
             )
 
-        def reduce_turns(c, i0, i1):
-            mc = CHUNKS[c][2]
-            if i0 == 0:
-                frac[c] = held.tile([P, PACK, mc], F32, name="frac%d" % c, tag="both1" if c == 2 else "frac%d" % c, align_bytes=64)
+        def reduce_turns(a, pair, m0=0, m1=M):
+            name = "frac%d%d" % (a, pair)
+            if m0 == 0:
+                frac[a, pair] = held.tile([P, 2, M], F32, name=name, tag="treble10" if (a, pair) == (1, 1) else name, align_bytes=64)
             nc.vector.scalar_tensor_tensor(
-                out=frac[c][:, i0:i1, :], in0=tenor[c][:, i0:i1, :], scalar=1.0 / (2.0 * math.pi),
-                in1=turns[c, i0][:], op0=ALU.mult, op1=ALU.subtract,
+                out=frac[a, pair][:, :, m0:m1], in0=tenor[a][:, 2 * pair : 2 * pair + 2, m0:m1],
+                scalar=1.0 / (2.0 * math.pi), in1=turns[a, pair][:, :, m0:m1], op0=ALU.mult, op1=ALU.subtract,
             )
 
-        def do_tanh(c, i0, i1):
-            nc.scalar.activation(treble[c][:, i0:i1, :], treble[c][:, i0:i1, :], ACT.Tanh)
-
-        def do_sin(c, i0, i1):
-            nc.scalar.activation(tenor[c][:, i0:i1, :], frac[c][:, i0:i1, :], ACT.Sin, scale=2.0 * math.pi)
+        def do_sin(a, pair, m0=0, m1=M):
+            nc.scalar.activation(tenor[a][:, 2 * pair : 2 * pair + 2, m0:m1], frac[a, pair][:, :, m0:m1],
+                                 ACT.Sin, scale=2.0 * math.pi)
 
         def scale_sin(c, i0, i1):
-            a, m0, mc, on_scalar = CHUNKS[c]
-            if on_scalar:
-                for i in range(i0, i1):
-                    nc.scalar.activation(tenor[c][:, i, :], tenor[c][:, i, :], ACT.Copy, scale=gain_t[:, a, i : i + 1])
+            a, m0, mc, unused = CHUNKS[c]
+            for i in range(i0, i1):
+                part = tenor[a][:, i, m0 : m0 + mc]
+                nc.scalar.activation(part, part, ACT.Copy, scale=gain_t[:, a, i : i + 1])
 
-        diff, zb = {}, {}
+        def gather_treble(c, i):
+            a, m0, mc, unused = CHUNKS[c]
+            if c == 1:
+                name = "treble1%d" % i
+                treble[c, i] = held.tile([P, mc], F32, name=name, tag=name, align_bytes=64)[:]
+            else:
+                if i == 0:
+                    treble[c] = held.tile([P, PACK, mc], F32, name="treble%d" % c, tag=TREBLE_TAG[c], align_bytes=64)
+                treble[c, i] = treble[c][:, i, :]
+            nc.vector.tensor_copy(treble[c, i], h[a, i][:].indirect(pos1_t[:, m0 // 16 : (m0 + mc) // 16]))
+
+        def do_tanh(c, i0, i1):
+            if c == 1:
+                for i in range(i0, i1):
+                    nc.scalar.activation(treble[c, i], treble[c, i], ACT.Tanh)
+            else:
+                nc.scalar.activation(treble[c][:, i0:i1, :], treble[c][:, i0:i1, :], ACT.Tanh)
 
         def difference(c, i0, i1):
             a, m0, mc, on_scalar = CHUNKS[c]
             if i0 == 0:
-                diff[c] = held.tile([P, PACK, mc], F32, name="diff%d" % c, tag="h13" if c == last - 1 else "diff%d" % c, align_bytes=64)
+                diff[c] = held.tile([P, PACK, mc], F32, name="diff%d" % c, tag=DIFF_TAG[c], align_bytes=64)
             if on_scalar:
                 for i in range(i0, i1):
                     nc.vector.scalar_tensor_tensor(
-                        out=diff[c][:, i, :], in0=treble[c][:, i, :], scalar=gain_t[:, a, i : i + 1],
-                        in1=tenor[c][:, i, :], op0=ALU.mult, op1=ALU.subtract,
+                        out=diff[c][:, i, :], in0=treble[c, i], scalar=gain_t[:, a, i : i + 1],
+                        in1=tenor[a][:, i, m0 : m0 + mc], op0=ALU.mult, op1=ALU.subtract,
                     )
             else:
-                nc.vector.tensor_tensor(diff[c][:, i0:i1, :], treble[c][:, i0:i1, :], tenor[c][:, i0:i1, :], ALU.subtract)
+                nc.vector.tensor_tensor(diff[c][:, i0:i1, :], treble[c][:, i0:i1, :],
+                                        tenor[a][:, i0:i1, m0 : m0 + mc], ALU.subtract)
 
         def interleave(c):
             a, m0, mc, on_scalar = CHUNKS[c]
@@ -230,7 +234,7 @@ def tile_list_string_unison_beats_kernel(
         def second_product(c):
             a, m0, mc, unused = CHUNKS[c]
             if a not in zq:
-                zq[a] = held.tile([P, M], U32, name="zq%d" % a, tag="turns2" if a == 0 else "zq1", align_bytes=64)
+                zq[a] = held.tile([P, M], U32, name="zq%d" % a, tag="h1%d" % (2 - a), align_bytes=64)
             nc.vector.quantize_mx(
                 out=zq[a][:, m0 : m0 + mc].bitcast(FP8X4),
                 scales=zs[a][:, m0 : m0 + mc],
@@ -256,96 +260,81 @@ def tile_list_string_unison_beats_kernel(
         def square(q):
             nc.scalar.activation(squares[:, q, :], ybank[q][:].rearrange("p n m -> p (n m)"), ACT.Square)
 
-        def gather_both(c, i):
-            gather_tenor(c, i)
-            gather_treble(c, i)
-
-        make_h(0, 0)
-        gather_both(0, 0)
-        make_h(0, 1)
-        gather_tenor(0, 1)
-        count_turns(0, 0, 2)
-        gather_treble(0, 1)
+        for t in range(2):
+            make_h(0, t)
+            gather_tenor(0, t)
+            gather_treble(0, t)
         cast_w(pieces[3], False, 0, 128)
+        reduce_turns(0, 0)
         quantize_w(1, 0, 0, 4)
-        reduce_turns(0, 0, 2)
         make_h(0, 2)
-        gather_both(0, 2)
+        gather_tenor(0, 2)
+        gather_treble(0, 2)
         cast_w(pieces[4], False, 0, 128)
         quantize_w(1, 1, 0, 2)
         quantize_w(1, 1, 2, 4)
         make_h(0, 3)
         gather_tenor(0, 3)
-        count_turns(0, 2, 4)
         gather_treble(0, 3)
-        do_sin(0, 0, 2)
+        do_sin(0, 0)
         do_tanh(0, 0, 2)
-        scale_sin(0, 0, 2)
-        reduce_turns(0, 2, 4)
-        difference(0, 0, 2)
+        reduce_turns(0, 1)
         for t in range(2):
             make_h(1, t)
             gather_tenor(1, t)
-            if t == 1:
-                count_turns(1, 0, 2)
             gather_treble(1, t)
-        do_sin(0, 2, 4)
+        scale_sin(0, 0, 2)
+        difference(0, 0, 2)
+        reduce_turns(1, 0)
+        do_sin(0, 1)
         do_tanh(0, 2, 4)
         scale_sin(0, 2, 4)
         difference(0, 2, 4)
         for t in range(2, PACK):
             make_h(1, t)
             gather_tenor(1, t)
-            if t == 3:
-                count_turns(1, 2, 4)
             gather_treble(1, t)
-        reduce_turns(1, 0, 2)
-        reduce_turns(1, 2, 4)
+        do_tanh(1, 0, 2)
+        do_sin(1, 0)
+        scale_sin(1, 0, 2)
         interleave(0)
-        for i in (0, 2):
-            do_sin(1, i, i + 2)
-            do_tanh(1, i, i + 2)
-            scale_sin(1, i, i + 2)
-        for t in range(PACK):
-            gather_tenor(2, t)
-        count_turns(2, 0, 4)
+        difference(1, 0, 2)
+        reduce_turns(1, 1, 0, 256)
+        reduce_turns(1, 1, 256, M)
+        do_tanh(1, 2, 4)
+        do_sin(1, 1, 0, 256)
+        do_sin(1, 1, 256, M)
+        scale_sin(1, 2, 4)
         for t in range(PACK):
             gather_treble(2, t)
-        difference(1, 0, 4)
         do_tanh(2, 0, 4)
+        difference(1, 2, 4)
         interleave(1)
-        reduce_turns(2, 0, 4)
-        do_sin(2, 0, 4)
+        for t in range(PACK):
+            gather_treble(3, t)
+        do_tanh(3, 0, 3)
+        do_tanh(3, 3, 4)
+        nc.scalar.activation(warm[:, 0:1], treble[3][:, 0, 0:1], ACT.Sqrt, bias=1.0, scale=0.0)
         second_product(0)
         multiply(0, (0, 1))
         second_product(1)
         multiply(1, (0, 1))
         multiply(0, (2, 3))
-        square(0)
-        square(1)
-        for t in range(PACK):
-            gather_tenor(3, t)
-        count_turns(3, 0, 4)
-        gather_treble(3, 0)
-        reduce_turns(3, 0, 4)
-        for t in range(1, PACK):
-            gather_treble(3, t)
-        do_sin(3, 0, 4)
-        do_tanh(3, 0, 4)
+        difference(3, 0, 4)
         difference(2, 0, 4)
+        interleave(3)
         interleave(2)
-        difference(last, 0, 4)
-        second_product(last - 1)
-        multiply(1, (2,))
-        interleave(last)
-        square(2)
-        second_product(last)
+        second_product(3)
         multiply(1, (3,))
+        second_product(2)
+        multiply(1, (2,))
 
-        result = held.tile([P, M // QUARTER, N // P, QUARTER], F32, name="result", tag="frac%d" % last, align_bytes=64)
+        result = held.tile([P, M // QUARTER, N // P, QUARTER], F32, name="result", align_bytes=64)
         out_view = out.rearrange("(n p) m -> p n m", p=P)
-        for q in range(M // QUARTER):
-            if q == M // QUARTER - 1:
+        for q in (0, 1, 3, 2):
+            if q != 1:
                 square(q)
+            if q == 0:
+                square(1)
             nc.scalar.activation(result[:, q].rearrange("p n m -> p (n m)"), squares[:, q, :], ACT.Sqrt, bias=1.0)
             nc.sync.dma_start(out=out_view[:, :, QUARTER * q : QUARTER * (q + 1)], in_=result[:, q])

@@ -19,7 +19,7 @@ ALU = mybir.AluOpType
 
 P = 128
 TREBLE_TAG = ["treble0", None, "treble11", "treble12"]
-DIFF_TAG = ["diff0", "diff1", "zb1", "diff3"]
+DIFF_TAG = ["diff0", "diff1", "h13", "diff3"]
 PACK = 4
 PASS = P * PACK
 BANK = 512
@@ -83,8 +83,8 @@ def tile_list_string_unison_beats_kernel(
             if (b, a) not in wb:
                 wb[b, a] = held.tile([P, PACK, P, PACK], BF16, name="wb%d%d" % (b, a),
                                      tag=reuse.get((b, a), "wb%d%d" % (b, a)), align_bytes=64)
-            dst = wb[b, a][:, :, m0 + lo : m0 + hi, :].rearrange("p t m j -> p m t j")
-            src = wraw[piece][:, :, PACK * lo : PACK * hi].rearrange("p j (m t) -> p m t j", t=PACK)
+            dst = wb[b, a][:, :, m0 + lo : m0 + hi, :].rearrange("p t m j -> p m j t")
+            src = wraw[piece][:, :, PACK * lo : PACK * hi].rearrange("p j (m t) -> p m j t", t=PACK)
             if on_vector:
                 nc.vector.tensor_copy(out=dst, in_=src)
             else:
@@ -109,13 +109,13 @@ def tile_list_string_unison_beats_kernel(
         load_w(pieces[3], "tabw0")
         load_w(pieces[4], "tabw1")
         w4w = held.tile([P, 2, 2 * N], U8, name="w4w", tag="wraw0", align_bytes=64)
-        cast_w(pieces[0], False, 0, 80)
-        cast_w(pieces[0], True, 80, 128)
+        cast_w(pieces[0], False, 0, 64)
+        cast_w(pieces[0], True, 64, 128)
         nc.sync.dma_start(out=w4w[:].bitcast(I32), in_=w4_words.rearrange("a p c -> p a c").bitcast(I32))
         cast_w(pieces[1], False, 0, 64)
         quantize_w(0, 0, 0, 4)
-        cast_w(pieces[2], False, 0, 32)
-        cast_w(pieces[2], True, 32, 64)
+        cast_w(pieces[2], False, 0, 24)
+        cast_w(pieces[2], True, 24, 64)
         for t in range(PACK):
             quantize_w(0, 1, t, t + 1)
 
@@ -164,7 +164,8 @@ def tile_list_string_unison_beats_kernel(
             name = "turns%d%d" % (a, i // 2)
             if i % 2 == 0:
                 turns[a, i // 2] = held.tile([P, 2, M], I32, name=name, tag=name, align_bytes=64)
-            nc.gpsimd.tensor_scalar(
+            engine = nc.vector if (a == 1 and i % 2 == 1) else nc.gpsimd
+            engine.tensor_scalar(
                 out=turns[a, i // 2][:, i % 2, :], in0=tenor[a][:, i, :],
                 scalar1=1.0 / (2.0 * math.pi), scalar2=0.0, op0=ALU.mult, op1=ALU.add,
             )
@@ -220,25 +221,27 @@ def tile_list_string_unison_beats_kernel(
                 nc.vector.tensor_tensor(diff[c][:, i0:i1, :], treble[c][:, i0:i1, :],
                                         tenor[a][:, i0:i1, m0 : m0 + mc], ALU.subtract)
 
-        def interleave(c):
+        def interleave(c, lo=0, hi=None):
             a, m0, mc, on_scalar = CHUNKS[c]
-            zb[c] = held.tile([P, mc, PACK], BF16, name="zb%d" % c, tag="zb%d" % c, align_bytes=64)
-            dst = zb[c][:].rearrange("p (c u) i -> p c i u", u=4)
-            src = diff[c][:].rearrange("p i (c u) -> p c i u", u=4)
+            if lo == 0:
+                zb[c] = held.tile([P, mc, PACK], BF16, name="zb%d" % c, tag="zb%d" % c, align_bytes=64)
+            dst = zb[c][:, lo:hi, :].rearrange("p (c u) i -> p c i u", u=4)
+            src = diff[c][:, :, lo:hi].rearrange("p i (c u) -> p c i u", u=4)
             if on_scalar:
                 nc.scalar.copy(out=dst, in_=src)
             else:
                 g = gain_t[:, a, :].rearrange("p (c i u) -> p c i u", c=1, u=1).broadcast_to([P, mc // 4, PACK, 4])
                 nc.vector.tensor_tensor(dst, src, g, ALU.mult)
 
-        def second_product(c):
+        def second_product(c, lo=0, hi=None):
             a, m0, mc, unused = CHUNKS[c]
+            hi = mc if hi is None else hi
             if a not in zq:
                 zq[a] = held.tile([P, M], U32, name="zq%d" % a, tag="h1%d" % (2 - a), align_bytes=64)
             nc.vector.quantize_mx(
-                out=zq[a][:, m0 : m0 + mc].bitcast(FP8X4),
-                scales=zs[a][:, m0 : m0 + mc],
-                in_=zb[c][:].rearrange("p m i -> p (m i)"),
+                out=zq[a][:, m0 + lo : m0 + hi].bitcast(FP8X4),
+                scales=zs[a][:, m0 + lo : m0 + hi],
+                in_=zb[c][:, lo:hi, :].rearrange("p m i -> p (m i)"),
             )
 
         def multiply(a, quarters):
@@ -297,7 +300,8 @@ def tile_list_string_unison_beats_kernel(
         do_tanh(1, 0, 2)
         do_sin(1, 0)
         scale_sin(1, 0, 2)
-        interleave(0)
+        interleave(0, 0, 256)
+        interleave(0, 256, M)
         difference(1, 0, 2)
         reduce_turns(1, 1, 0, 256)
         reduce_turns(1, 1, 256, M)
@@ -315,26 +319,25 @@ def tile_list_string_unison_beats_kernel(
         do_tanh(3, 0, 3)
         do_tanh(3, 3, 4)
         nc.scalar.activation(warm[:, 0:1], treble[3][:, 0, 0:1], ACT.Sqrt, bias=1.0, scale=0.0)
-        second_product(0)
-        multiply(0, (0, 1))
+        second_product(0, 0, 256)
         second_product(1)
-        multiply(1, (0, 1))
-        multiply(0, (2, 3))
-        difference(3, 0, 4)
+        for q in range(2):
+            multiply(0, (q,))
+            multiply(1, (q,))
         difference(2, 0, 4)
-        interleave(3)
+        second_product(0, 256, M)
+        multiply(0, (2, 3))
         interleave(2)
-        second_product(3)
-        multiply(1, (3,))
+        difference(3, 0, 4)
         second_product(2)
         multiply(1, (2,))
+        interleave(3)
+        second_product(3)
+        multiply(1, (3,))
 
         result = held.tile([P, M // QUARTER, N // P, QUARTER], F32, name="result", align_bytes=64)
         out_view = out.rearrange("(n p) m -> p n m", p=P)
-        for q in (0, 1, 3, 2):
-            if q != 1:
-                square(q)
-            if q == 0:
-                square(1)
+        for q in range(M // QUARTER):
+            square(q)
             nc.scalar.activation(result[:, q].rearrange("p n m -> p (n m)"), squares[:, q, :], ACT.Sqrt, bias=1.0)
             nc.sync.dma_start(out=out_view[:, :, QUARTER * q : QUARTER * (q + 1)], in_=result[:, q])

import math
from contextlib import ExitStack

import concourse.mybir as mybir

T, S, M, K, H, N = 4096, 1024, 512, 1024, 1024, 512
FLOPS = 2 * K * H * S + 2 * H * N * M

F32 = mybir.dt.float32
BF16 = mybir.dt.bfloat16
I32 = mybir.dt.int32
U32 = mybir.dt.uint32
U16 = mybir.dt.uint16
U8 = mybir.dt.uint8
FP8X4 = mybir.dt.float8_e4m3fn_x4
FP4X4 = mybir.dt.float4_e2m1fn_x4
ACT = mybir.ActivationFunctionType
ALU = mybir.AluOpType

P = 128
TREBLE_TAG = ["treble0", None, "treble11", "treble12"]
DIFF_TAG = ["diff0", "diff1", "h13", "diff3"]
PACK = 4
PASS = P * PACK
BANK = 512
QUARTER = 128

CHUNKS = [(0, 0, 512, True), (1, 0, 256, True), (1, 256, 128, False), (1, 384, 128, False)]


def tile_list_string_unison_beats_kernel(
    tc, tab_words, tab_scales, offs, pos1, pos2, w1, gain, w4_words, w4_scales, out
):
    nc = tc.nc
    with ExitStack() as ctx:
        held = ctx.enter_context(tc.tile_pool(name="held", bufs=1))
        hpsum = ctx.enter_context(tc.psum_pool(name="hpsum", bufs=4))
        ypsum = ctx.enter_context(tc.psum_pool(name="ypsum", bufs=1))

        offs_t = held.tile([P, S // 16], U16, name="offs_t")
        pos1_t = held.tile([P, M // 16], U16, name="pos1_t")
        pos2_t = held.tile([P, M // 16], U16, name="pos2_t")
        tabw = [held.tile([P, T], U16, name="tabw%d" % a, tag="tabw%d" % a, align_bytes=64) for a in range(2)]
        tabs = held.tile([P, T], U8, name="tabs", tag="tabs", align_bytes=64)
        vw = [held.tile([P, S], U16, name="vw%d" % a, align_bytes=64) for a in range(2)]
        picked = held.tile([P, S], U8, name="picked", align_bytes=64)
        vs = held.tile([P, 2, S], U8, name="vs", align_bytes=64)
        warm = held.tile([P, 2], F32, name="warm")

        nc.vector.memset(warm[:, 0:1], 0.0)
        nc.vector.memset(tabs[32:64, :].bitcast(I32), 0)
        nc.vector.memset(tabs[64:128, :].bitcast(I32), 0)
        nc.vector.memset(vs[:].rearrange("p a n -> p (a n)").bitcast(I32), 0)
        nc.scalar.activation(warm[:, 1:2], warm[:, 0:1], ACT.Silu)

        pieces = [(0, 0, 0, 128), (0, 1, 0, 64), (0, 1, 64, 64), (1, 0, 0, 128), (1, 1, 0, 128)]
        wraw = {}

        def load_w(piece, tag):
            b, a, m0, mc = piece
            raw = held.tile([P, PACK, PACK * mc], F32, name="wraw%d%d%d" % (b, a, m0), tag=tag, align_bytes=64)
            c0 = PASS * b + PACK * m0
            rows = w1[PASS * a : PASS * (a + 1), c0 : c0 + PACK * mc]
            nc.sync.dma_start(out=raw[:], in_=rows.rearrange("(p j) c -> p j c", j=PACK))
            wraw[piece] = raw

        nc.sync.dma_start(offs_t[:], offs)
        nc.sync.dma_start(pos2_t[:], pos2)
        nc.sync.dma_start(pos1_t[:], pos1)
        nc.sync.dma_start(out=tabs[0:32, :].bitcast(I32), in_=tab_scales.rearrange("a q t -> q a t").bitcast(I32))
        for a in range(2):
            nc.sync.dma_start(out=tabw[a][:].bitcast(I32), in_=tab_words[a].bitcast(I32))
        for n in range(3):
            load_w(pieces[n], "wraw%d" % n)

        wb, wq = {}, {}
        reuse = {(1, 0): "wq011", (1, 1): "wq012"}
        ws = {(b, a): held.tile([P, PASS], U8, name="ws%d%d" % (b, a), align_bytes=64)
              for b in range(2) for a in range(2)}

        def cast_w(piece, on_vector, lo, hi):
            b, a, m0, mc = piece
            if (b, a) not in wb:
                wb[b, a] = held.tile([P, PACK, P, PACK], BF16, name="wb%d%d" % (b, a),
                                     tag=reuse.get((b, a), "wb%d%d" % (b, a)), align_bytes=64)
            dst = wb[b, a][:, :, m0 + lo : m0 + hi, :].rearrange("p t m j -> p m j t")
            src = wraw[piece][:, :, PACK * lo : PACK * hi].rearrange("p j (m t) -> p m j t", t=PACK)
            if on_vector:
                nc.vector.tensor_copy(out=dst, in_=src)
            else:
                nc.scalar.copy(out=dst, in_=src)

        def quantize_w(b, a, t0, t1):
            name = "wq%d%d%d" % (b, a, t0)
            codes = held.tile([P, P * (t1 - t0)], U32, name=name, tag=name, align_bytes=64)
            for t in range(t0, t1):
                wq[b, a, t] = codes[:, P * (t - t0) : P * (t - t0 + 1)]
            nc.vector.quantize_mx(
                out=codes[:].bitcast(FP8X4),
                scales=ws[b, a][:, P * t0 : P * t1],
                in_=wb[b, a][:, t0:t1, :, :].rearrange("p t m j -> p (t m j)"),
            )

        nc.vector.tensor_copy(picked[:], tabs[:].indirect(offs_t[:]))
        for q in range(4):
            nc.scalar.dma_start(out=vs[32 * q : 32 * q + 4, :, :].bitcast(I32), in_=picked[8 * q : 8 * q + 8, :].bitcast(I32))
        for a in range(2):
            nc.vector.tensor_copy(vw[a][:], tabw[a][:].indirect(offs_t[:]))
        load_w(pieces[3], "tabw0")
        load_w(pieces[4], "tabw1")
        w4w = held.tile([P, 2, 2 * N], U8, name="w4w", tag="wraw0", align_bytes=64)
        cast_w(pieces[0], False, 0, 64)
        cast_w(pieces[0], True, 64, 128)
        nc.sync.dma_start(out=w4w[:].bitcast(I32), in_=w4_words.rearrange("a p c -> p a c").bitcast(I32))
        cast_w(pieces[1], False, 0, 64)
        quantize_w(0, 0, 0, 4)
        cast_w(pieces[2], False, 0, 24)
        cast_w(pieces[2], True, 24, 64)
        for t in range(PACK):
            quantize_w(0, 1, t, t + 1)

        gain_t = held.tile([P, 2, PACK], F32, name="gain_t", tag="wraw1", align_bytes=64)
        w4s = held.tile([P, 2, N], U8, name="w4s", tag="wraw2", align_bytes=64)
        nc.vector.memset(w4s[:].rearrange("p a n -> p (a n)").bitcast(I32), 0)
        nc.sync.dma_start(out=gain_t[:], in_=gain.rearrange("(a p i) -> p a i", a=2, i=PACK))
        for q in range(4):
            nc.sync.dma_start(
                out=w4s[32 * q : 32 * q + 4, :, :].bitcast(I32),
                in_=w4_scales[:, 4 * q : 4 * q + 4, :].rearrange("a r n -> r a n").bitcast(I32),
            )

        h = {}

        def make_h(b, t):
            tile = held.tile([P, S], F32, name="h%d%d" % (b, t), tag="h%d%d" % (b, t), align_bytes=64)
            for half in range(2):
                cols = slice(BANK * half, BANK * (half + 1))
                acc = hpsum.tile([P, BANK], F32, name="hacc")
                for a in range(2):
                    nc.tensor.matmul_mx(
                        out=acc[:],
                        lhsT=wq[b, a, t].bitcast(FP8X4),
                        lhsT_scale=ws[b, a][:, P * t : P * (t + 1)],
                        rhs=vw[a][:, cols].bitcast(FP4X4),
                        rhs_scale=vs[:, a, cols],
                        start=(a == 0),
                        stop=(a == 1),
                    )
                if (b, t, half) == (0, 0, 1):
                    nc.vector.tensor_copy(out=tile[:, cols], in_=acc[:])
                else:
                    nc.scalar.copy(out=tile[:, cols], in_=acc[:])
            h[b, t] = tile

        zq = {}
        zs = [held.tile([P, M], U8, name="zs%d" % a, align_bytes=64) for a in range(2)]
        ybank = [ypsum.tile([P, N // P, QUARTER], F32, name="y%d" % q) for q in range(M // QUARTER)]
        last = len(CHUNKS) - 1
        tenor = [held.tile([P, PACK, M], F32, name="tenor%d" % a) for a in range(2)]
        turns, frac, treble, diff, zb = {}, {}, {}, {}, {}

        def gather_tenor(a, i):
            nc.vector.tensor_copy(tenor[a][:, i, :], h[a, i][:].indirect(pos2_t[:]))
            name = "turns%d%d" % (a, i // 2)
            if i % 2 == 0:
                turns[a, i // 2] = held.tile([P, 2, M], I32, name=name, tag=name, align_bytes=64)
            engine = nc.vector if (a == 1 and i % 2 == 1) else nc.gpsimd
            engine.tensor_scalar(
                out=turns[a, i // 2][:, i % 2, :], in0=tenor[a][:, i, :],
                scalar1=1.0 / (2.0 * math.pi), scalar2=0.0, op0=ALU.mult, op1=ALU.add,
            )

        def reduce_turns(a, pair, m0=0, m1=M):
            name = "frac%d%d" % (a, pair)
            if m0 == 0:
                frac[a, pair] = held.tile([P, 2, M], F32, name=name, tag="treble10" if (a, pair) == (1, 1) else name, align_bytes=64)
            nc.vector.scalar_tensor_tensor(
                out=frac[a, pair][:, :, m0:m1], in0=tenor[a][:, 2 * pair : 2 * pair + 2, m0:m1],
                scalar=1.0 / (2.0 * math.pi), in1=turns[a, pair][:, :, m0:m1], op0=ALU.mult, op1=ALU.subtract,
            )

        def do_sin(a, pair, m0=0, m1=M):
            nc.scalar.activation(tenor[a][:, 2 * pair : 2 * pair + 2, m0:m1], frac[a, pair][:, :, m0:m1],
                                 ACT.Sin, scale=2.0 * math.pi)

        def scale_sin(c, i0, i1):
            a, m0, mc, unused = CHUNKS[c]
            for i in range(i0, i1):
                part = tenor[a][:, i, m0 : m0 + mc]
                nc.scalar.activation(part, part, ACT.Copy, scale=gain_t[:, a, i : i + 1])

        def gather_treble(c, i):
            a, m0, mc, unused = CHUNKS[c]
            if c == 1:
                name = "treble1%d" % i
                treble[c, i] = held.tile([P, mc], F32, name=name, tag=name, align_bytes=64)[:]
            else:
                if i == 0:
                    treble[c] = held.tile([P, PACK, mc], F32, name="treble%d" % c, tag=TREBLE_TAG[c], align_bytes=64)
                treble[c, i] = treble[c][:, i, :]
            nc.vector.tensor_copy(treble[c, i], h[a, i][:].indirect(pos1_t[:, m0 // 16 : (m0 + mc) // 16]))

        def do_tanh(c, i0, i1):
            if c == 1:
                for i in range(i0, i1):
                    nc.scalar.activation(treble[c, i], treble[c, i], ACT.Tanh)
            else:
                nc.scalar.activation(treble[c][:, i0:i1, :], treble[c][:, i0:i1, :], ACT.Tanh)

        def difference(c, i0, i1):
            a, m0, mc, on_scalar = CHUNKS[c]
            if i0 == 0:
                diff[c] = held.tile([P, PACK, mc], F32, name="diff%d" % c, tag=DIFF_TAG[c], align_bytes=64)
            if on_scalar:
                for i in range(i0, i1):
                    nc.vector.scalar_tensor_tensor(
                        out=diff[c][:, i, :], in0=treble[c, i], scalar=gain_t[:, a, i : i + 1],
                        in1=tenor[a][:, i, m0 : m0 + mc], op0=ALU.mult, op1=ALU.subtract,
                    )
            else:
                nc.vector.tensor_tensor(diff[c][:, i0:i1, :], treble[c][:, i0:i1, :],
                                        tenor[a][:, i0:i1, m0 : m0 + mc], ALU.subtract)

        def interleave(c, lo=0, hi=None):
            a, m0, mc, on_scalar = CHUNKS[c]
            if lo == 0:
                zb[c] = held.tile([P, mc, PACK], BF16, name="zb%d" % c, tag="zb%d" % c, align_bytes=64)
            dst = zb[c][:, lo:hi, :].rearrange("p (c u) i -> p c i u", u=4)
            src = diff[c][:, :, lo:hi].rearrange("p i (c u) -> p c i u", u=4)
            if on_scalar:
                nc.scalar.copy(out=dst, in_=src)
            else:
                g = gain_t[:, a, :].rearrange("p (c i u) -> p c i u", c=1, u=1).broadcast_to([P, mc // 4, PACK, 4])
                nc.vector.tensor_tensor(dst, src, g, ALU.mult)

        def second_product(c, lo=0, hi=None):
            a, m0, mc, unused = CHUNKS[c]
            hi = mc if hi is None else hi
            if a not in zq:
                zq[a] = held.tile([P, M], U32, name="zq%d" % a, tag="h1%d" % (2 - a), align_bytes=64)
            nc.vector.quantize_mx(
                out=zq[a][:, m0 + lo : m0 + hi].bitcast(FP8X4),
                scales=zs[a][:, m0 + lo : m0 + hi],
                in_=zb[c][:, lo:hi, :].rearrange("p m i -> p (m i)"),
            )

        def multiply(a, quarters):
            for q in quarters:
                cols = slice(QUARTER * q, QUARTER * (q + 1))
                for n in range(N // P):
                    nc.tensor.matmul_mx(
                        out=ybank[q][:, n, :],
                        lhsT=w4w[:, a, 2 * P * n : 2 * P * (n + 1)].bitcast(FP4X4),
                        lhsT_scale=w4s[:, a, P * n : P * (n + 1)],
                        rhs=zq[a][:, cols].bitcast(FP8X4),
                        rhs_scale=zs[a][:, cols],
                        start=(a == 0 and n == 0),
                        stop=(a == 1 and n == N // P - 1),
                    )

        squares = held.tile([P, M // QUARTER, BANK], F32, name="squares")

        def square(q):
            nc.scalar.activation(squares[:, q, :], ybank[q][:].rearrange("p n m -> p (n m)"), ACT.Square)

        for t in range(2):
            make_h(0, t)
            gather_tenor(0, t)
            gather_treble(0, t)
        cast_w(pieces[3], False, 0, 128)
        reduce_turns(0, 0)
        quantize_w(1, 0, 0, 4)
        make_h(0, 2)
        gather_tenor(0, 2)
        gather_treble(0, 2)
        cast_w(pieces[4], False, 0, 128)
        quantize_w(1, 1, 0, 2)
        quantize_w(1, 1, 2, 4)
        make_h(0, 3)
        gather_tenor(0, 3)
        gather_treble(0, 3)
        do_sin(0, 0)
        do_tanh(0, 0, 2)
        reduce_turns(0, 1)
        for t in range(2):
            make_h(1, t)
            gather_tenor(1, t)
            gather_treble(1, t)
        scale_sin(0, 0, 2)
        difference(0, 0, 2)
        reduce_turns(1, 0)
        do_sin(0, 1)
        do_tanh(0, 2, 4)
        scale_sin(0, 2, 4)
        difference(0, 2, 4)
        for t in range(2, PACK):
            make_h(1, t)
            gather_tenor(1, t)
            gather_treble(1, t)
        do_tanh(1, 0, 2)
        do_sin(1, 0)
        scale_sin(1, 0, 2)
        interleave(0, 0, 256)
        interleave(0, 256, M)
        difference(1, 0, 2)
        reduce_turns(1, 1, 0, 256)
        reduce_turns(1, 1, 256, M)
        do_tanh(1, 2, 4)
        do_sin(1, 1, 0, 256)
        do_sin(1, 1, 256, M)
        scale_sin(1, 2, 4)
        for t in range(PACK):
            gather_treble(2, t)
        do_tanh(2, 0, 4)
        difference(1, 2, 4)
        interleave(1)
        for t in range(PACK):
            gather_treble(3, t)
        do_tanh(3, 0, 3)
        do_tanh(3, 3, 4)
        nc.scalar.activation(warm[:, 0:1], treble[3][:, 0, 0:1], ACT.Sqrt, bias=1.0, scale=0.0)
        second_product(0, 0, 256)
        second_product(1)
        for q in range(2):
            multiply(0, (q,))
            multiply(1, (q,))
        difference(2, 0, 4)
        second_product(0, 256, M)
        multiply(0, (2, 3))
        interleave(2)
        difference(3, 0, 4)
        second_product(2)
        multiply(1, (2,))
        interleave(3)
        second_product(3)
        multiply(1, (3,))

        result = held.tile([P, M // QUARTER, N // P, QUARTER], F32, name="result", align_bytes=64)
        out_view = out.rearrange("(n p) m -> p n m", p=P)
        for q in range(M // QUARTER):
            square(q)
            nc.scalar.activation(result[:, q].rearrange("p n m -> p (n m)"), squares[:, q, :], ACT.Sqrt, bias=1.0)
            nc.sync.dma_start(out=out_view[:, :, QUARTER * q : QUARTER * (q + 1)], in_=result[:, q])
